import numpy as np
import ml_dtypes


def mxq(x, axis, fmt="e4m3"):
    dtype, down = {"e4m3": (ml_dtypes.float8_e4m3fn, 7), "e5m2": (ml_dtypes.float8_e5m2, 14)}[fmt]
    v = np.moveaxis(np.asarray(x, np.float32).astype(ml_dtypes.bfloat16).astype(np.float64), axis, -1)
    blocks = v.reshape(v.shape[:-1] + (-1, 32))
    amax = np.abs(blocks).max(-1, keepdims=True)
    byte = np.maximum(np.where(amax > 0, np.frexp(amax)[1] - 1 + 127, 0) - down, 1)
    scale = np.exp2(byte - 127.0)
    codes = (blocks / scale).astype(np.float32).astype(dtype).astype(np.float64)
    return np.moveaxis((codes * scale).reshape(v.shape), -1, axis)


WIDE = False


def mx_kscale(k):
    if not WIDE:
        return np.ones(k)
    levels = np.array([10, -10, 5, -5, 0])
    if k % 512:
        return np.exp2(np.random.permutation(np.resize(levels, k // 32))).repeat(32)
    a = np.empty((k // 512, 16))
    for p in range(k // 512):
        a[p, :8] = np.random.permutation(np.resize(levels, 8))
        for g in range(8):
            far = levels[np.abs(levels - a[p, g]) >= 10]
            a[p, g + 8] = far[np.random.randint(len(far))]
    return np.exp2(a.ravel()).repeat(32)


def f64(x):
    return np.asarray(x).astype(np.float64)


def striped(idx):
    return np.tile(idx.reshape(-1, 16).T, (8, 1)).astype(np.uint16)


def unstriped(offs):
    return offs[:16].T.reshape(-1).astype(np.int64)


def silu(v):
    return v / (1.0 + np.exp(-np.maximum(v, -700.0)))


K, T, S, V, H, N, J, U = 512, 2048, 512, 256, 512, 256, 512, 512


def setup_inputs():
    n = np.random.standard_normal
    s = mx_kscale(K)[:, None]
    u = mx_kscale(H)
    r = mx_kscale(J)[:, None]
    return {
        "xT": (n((K, T)) * s).astype(np.float32),
        "aT": (n((J, U)) * r).astype(np.float32),
        "w1": (n((K, H)) / np.sqrt(K) / s * u).astype(np.float32),
        "w3": (n((J, H)) / np.sqrt(J) / r).astype(np.float32),
        "w2": (n((H, N)) / np.sqrt(2 * H) / u[:, None]).astype(np.float32),
        "offs": striped(np.random.permutation(T)[:S]),
        "pos1": striped(np.random.permutation(S)[:V]),
        "pos2": striped(np.random.permutation(S)[:V]),
    }


def reference(xT, aT, w1, w3, w2, offs, pos1, pos2):
    xq = mxq(f64(xT)[:, unstriped(offs)], 0, "e4m3")
    h = silu(mxq(f64(w1), 0, "e4m3").T @ xq)
    f = mxq(f64(w3), 0, "e4m3").T @ mxq(f64(aT), 0, "e4m3")
    z = h[:, unstriped(pos1)] * f[:, :V] + h[:, unstriped(pos2)] * f[:, V:2 * V]
    return silu(mxq(f64(w2), 0, "e4m3").T @ mxq(z, 0, "e4m3"))

@@ -1,0 +1,176 @@
+from contextlib import ExitStack
+
+import concourse.mybir as mybir
+
+K, T, S, V, H, N = 512, 2048, 512, 256, 512, 256
+FLOPS = 2 * K * H * S + 2 * K * H * S + 2 * H * N * V
+
+F32 = mybir.dt.float32
+BF16 = mybir.dt.bfloat16
+U32 = mybir.dt.uint32
+U16 = mybir.dt.uint16
+U8 = mybir.dt.uint8
+FP8X4 = mybir.dt.float8_e4m3fn_x4
+SILU = mybir.ActivationFunctionType.Silu
+MULT = mybir.AluOpType.mult
+ADD = mybir.AluOpType.add
+
+P = 128
+PACK = 4
+HALF = 256
+
+
+def tile_picked_dime_silu_e_kernel(tc, xT, aT, w1, w3, w2, offs, pos1, pos2, out):
+    nc = tc.nc
+
+    with ExitStack() as ctx:
+        lists = ctx.enter_context(tc.tile_pool(name="lists", bufs=1))
+        sb = ctx.enter_context(tc.tile_pool(name="sb", bufs=1))
+        psum = ctx.enter_context(tc.psum_pool(name="psum", bufs=1))
+
+        def quantize(name, grouped, codes, scales):
+            nc.vector.quantize_mx(out=codes.bitcast(FP8X4), scales=scales, in_=grouped)
+
+        def mx_tiles(name, width):
+            codes = sb.tile([P, width], U32, name=name + "_codes", align_bytes=64)
+            scales = sb.tile([P, width], U8, name=name + "_scales", align_bytes=64)
+            return codes, scales
+
+        def product(acc, lhs, lhs_cols, rhs):
+            nc.tensor.matmul_mx(
+                out=acc,
+                lhsT=lhs[0][:, lhs_cols].bitcast(FP8X4),
+                lhsT_scale=lhs[1][:, lhs_cols],
+                rhs=rhs[0][:].bitcast(FP8X4),
+                rhs_scale=rhs[1][:],
+                start=True,
+                stop=True,
+            )
+
+        def load_half(name, src, half):
+            raw = sb.tile([P, PACK, HALF], F32, name="%s_raw%d" % (name, half))
+            nc.sync.dma_start(
+                out=raw[:], in_=src.rearrange("(p j) c -> p j c", j=PACK)[:, :, half * HALF : (half + 1) * HALF]
+            )
+            return raw
+
+        def copy_on(engine, dst, src):
+            if engine == "scalar":
+                nc.scalar.copy(out=dst, in_=src)
+            else:
+                nc.vector.tensor_copy(out=dst, in_=src)
+
+        def group_plain(name, raw, engine):
+            grouped = sb.tile([P, HALF * PACK], BF16, name=name, align_bytes=64)
+            copy_on(
+                engine,
+                grouped[:].rearrange("p (c i j) -> p c j i", i=4, j=PACK),
+                raw[:].rearrange("p j (c i) -> p c j i", i=4),
+            )
+            return grouped
+
+        def group_dealt(name, raw, engine):
+            grouped = sb.tile([P, HALF * PACK], BF16, name=name, align_bytes=64)
+            copy_on(
+                engine,
+                grouped[:].rearrange("p (t m j) -> p m j t", t=PACK, j=PACK),
+                raw[:].rearrange("p j (m t) -> p m j t", t=PACK),
+            )
+            return grouped
+
+        def quantize_dealt(grouped, half, t, target):
+            cols = slice(t * P + half * 64, t * P + (half + 1) * 64)
+            quantize("", grouped[:, t * HALF : (t + 1) * HALF], target[0][:, cols], target[1][:, cols])
+
+        x_rows = xT.rearrange("(p j) c -> p j c", j=PACK)
+        x_planes = [sb.tile([P, T], F32, name="x_plane%d" % j) for j in range(PACK)]
+        offs_sb = lists.tile([P, S // 16], U16, name="offs_sb")
+        pos1_sb = lists.tile([P, V // 16], U16, name="pos1_sb")
+        pos2_sb = lists.tile([P, V // 16], U16, name="pos2_sb")
+        nc.sync.dma_start(out=x_planes[0][:], in_=x_rows[:, 0, :])
+        nc.sync.dma_start(offs_sb[:], offs)
+        for j in range(1, PACK):
+            nc.sync.dma_start(out=x_planes[j][:], in_=x_rows[:, j, :])
+        w1_raw = [load_half("w1", w1, half) for half in range(2)]
+        nc.sync.dma_start(pos1_sb[:], pos1)
+        nc.sync.dma_start(pos2_sb[:], pos2)
+        a_raw = [load_half("a", aT, half) for half in range(2)]
+        w3_raw = sb.tile([P, PACK, H], F32, name="w3_raw")
+        nc.sync.dma_start(out=w3_raw[:], in_=w3.rearrange("(p j) c -> p j c", j=PACK))
+        w2_raw = load_half("w2", w2, 0)
+
+        x_grouped = sb.tile([P, S, PACK], BF16, name="x_grouped", align_bytes=64)
+        for j in range(PACK):
+            nc.vector.tensor_copy(x_grouped[:, :, j], x_planes[j][:].indirect(offs_sb[:]))
+        w1_grouped0 = group_dealt("w1_grouped0", w1_raw[0], "scalar")
+        x_mx = mx_tiles("x", S)
+        quantize("", x_grouped[:].rearrange("p s j -> p (s j)"), x_mx[0][:], x_mx[1][:])
+        w1_grouped1 = group_dealt("w1_grouped1", w1_raw[1], "vector")
+        w1_mx = [mx_tiles("w1_%d" % t, P) for t in range(PACK)]
+        for t in range(PACK):
+            quantize("", w1_grouped0[:, t * HALF : (t + 1) * HALF], w1_mx[t][0][:, 0:64], w1_mx[t][1][:, 0:64])
+        for t in range(PACK):
+            quantize("", w1_grouped1[:, t * HALF : (t + 1) * HALF], w1_mx[t][0][:, 64:128], w1_mx[t][1][:, 64:128])
+
+        a_grouped0 = group_plain("a_grouped0", a_raw[0], "scalar")
+
+        h_banks = [psum.tile([P, S], F32, name="h_bank%d" % t, tag="bank%d" % t) for t in range(PACK)]
+        h = [sb.tile([P, S], F32, name="h%d" % t) for t in range(PACK)]
+        for t in range(PACK):
+            product(h_banks[t][:], w1_mx[t], slice(0, P), x_mx)
+            nc.scalar.activation(out=h[t][:], in_=h_banks[t][:], func=SILU)
+
+        a_grouped1 = group_plain("a_grouped1", a_raw[1], "vector")
+        a_mx = mx_tiles("a", S)
+        w3_grouped = sb.tile([P, PACK, P, PACK], BF16, name="w3_grouped", tag="w3_then_picked", align_bytes=64)
+        nc.scalar.copy(
+            out=w3_grouped[:].rearrange("p t m j -> p m j t"),
+            in_=w3_raw[:].rearrange("p j (m t) -> p m j t", t=PACK),
+        )
+        w2_grouped = group_plain("w2_grouped", w2_raw, "scalar")
+        w3_mx = [mx_tiles("w3_%d" % t, P) for t in range(PACK)]
+
+        picked = [sb.tile([P, 2 * V], F32, name="picked%d" % t) for t in range(PACK - 1)]
+
+        def fetch(t):
+            nc.vector.tensor_copy(picked[t][:, 0:V], h[t][:].indirect(pos1_sb[:]))
+            nc.vector.tensor_copy(picked[t][:, V : 2 * V], h[t][:].indirect(pos2_sb[:]))
+
+        fetch(0)
+        quantize("", a_grouped0[:], a_mx[0][:, 0:HALF], a_mx[1][:, 0:HALF])
+        quantize("", a_grouped1[:], a_mx[0][:, HALF:S], a_mx[1][:, HALF:S])
+        fetch(1)
+        fetch(2)
+        for t in range(PACK):
+            quantize("", w3_grouped[:, t, :, :].rearrange("p m j -> p (m j)"), w3_mx[t][0][:], w3_mx[t][1][:])
+        picked.append(sb.tile([P, 2 * V], F32, name="picked3", tag="w3_then_picked", align_bytes=64))
+        fetch(3)
+
+        f_banks = [psum.tile([P, S], F32, name="f_bank%d" % t, tag="bank%d" % (PACK + t)) for t in range(PACK)]
+        terms = sb.tile([P, PACK, 2 * V], F32, name="terms")
+        for t in range(PACK):
+            product(f_banks[t][:], w3_mx[t], slice(0, P), a_mx)
+            nc.vector.tensor_tensor(terms[:, t, :], picked[t][:], f_banks[t][:], MULT)
+
+        w2_mx = mx_tiles("w2", N)
+        quantize("", w2_grouped[:], w2_mx[0][:], w2_mx[1][:])
+
+        VH = V // 2
+        z_grouped = [sb.tile([P, VH * PACK], BF16, name="z_grouped%d" % half, align_bytes=64) for half in range(2)]
+        for half in range(2):
+            nc.vector.tensor_tensor(
+                z_grouped[half][:].rearrange("p (c i t) -> p c t i", i=4, t=PACK),
+                terms[:, :, half * VH : (half + 1) * VH].rearrange("p t (c i) -> p c t i", i=4),
+                terms[:, :, V + half * VH : V + (half + 1) * VH].rearrange("p t (c i) -> p c t i", i=4),
+                ADD,
+            )
+        out_rows = out.rearrange("(u p) v -> p u v", p=P)
+        for half in range(2):
+            z_mx = mx_tiles("z%d" % half, VH)
+            quantize("", z_grouped[half][:], z_mx[0][:], z_mx[1][:])
+            o_bank = psum.tile([P, N // P, VH], F32, name="o_bank%d" % half, tag="bank%d" % half)
+            for u in range(N // P):
+                product(o_bank[:, u, :], w2_mx, slice(u * P, (u + 1) * P), z_mx)
+            result = sb.tile([P, N // P, VH], F32, name="result%d" % half)
+            nc.scalar.activation(out=result[:], in_=o_bank[:], func=SILU)
+            nc.sync.dma_start(out=out_rows[:, :, half * VH : (half + 1) * VH], in_=result[:])

@@ -92,12 +92,29 @@ def tile_picked_dime_silu_e_kernel(tc, xT, aT, w1, w3, w2, offs, pos1, pos2, out
         for j in range(1, PACK):
             nc.sync.dma_start(out=x_planes[j][:], in_=x_rows[:, j, :])
         w1_raw = [load_half("w1", w1, half) for half in range(2)]
-        nc.sync.dma_start(pos1_sb[:], pos1)
-        nc.sync.dma_start(pos2_sb[:], pos2)
-        a_raw = [load_half("a", aT, half) for half in range(2)]
+        a_rows = aT.rearrange("(p j) c -> p j c", j=PACK)
+        a_raw = [sb.tile([P, PACK, P], F32, name="a_raw%d" % q) for q in range(4)]
+        for q in range(4):
+            if q == 2:
+                nc.sync.dma_start(pos1_sb[:], pos1)
+                nc.sync.dma_start(pos2_sb[:], pos2)
+            nc.sync.dma_start(out=a_raw[q][:], in_=a_rows[:, :, q * P : (q + 1) * P])
+        a_grouped = [sb.tile([P, 2, P * PACK], BF16, name="a_grouped%d" % d, align_bytes=64) for d in range(2)]
+
+        def group_angles(q, engine):
+            copy_on(
+                engine,
+                a_grouped[q // 2][:, q % 2, :].rearrange("p (c i j) -> p c j i", i=4, j=PACK),
+                a_raw[q][:].rearrange("p j (c i) -> p c j i", i=4),
+            )
+
         w3_raw = sb.tile([P, PACK, H], F32, name="w3_raw")
         nc.sync.dma_start(out=w3_raw[:], in_=w3.rearrange("(p j) c -> p j c", j=PACK))
         w2_raw = load_half("w2", w2, 0)
+
+        warm = sb.tile([P, 16], F32, name="warm")
+        nc.vector.memset(warm[:, 0:1], 0.0)
+        nc.scalar.activation(out=warm[:, 8:9], in_=warm[:, 0:1], func=SILU)
 
         x_grouped = sb.tile([P, S, PACK], BF16, name="x_grouped", align_bytes=64)
         for j in range(PACK):
@@ -107,12 +124,14 @@ def tile_picked_dime_silu_e_kernel(tc, xT, aT, w1, w3, w2, offs, pos1, pos2, out
         quantize("", x_grouped[:].rearrange("p s j -> p (s j)"), x_mx[0][:], x_mx[1][:])
         w1_grouped1 = group_dealt("w1_grouped1", w1_raw[1], "vector")
         w1_mx = [mx_tiles("w1_%d" % t, P) for t in range(PACK)]
-        for t in range(PACK):
-            quantize("", w1_grouped0[:, t * HALF : (t + 1) * HALF], w1_mx[t][0][:, 0:64], w1_mx[t][1][:, 0:64])
-        for t in range(PACK):
-            quantize("", w1_grouped1[:, t * HALF : (t + 1) * HALF], w1_mx[t][0][:, 64:128], w1_mx[t][1][:, 64:128])
+        for pair in range(2):
+            for half, grouped in enumerate((w1_grouped0, w1_grouped1)):
+                for t in (2 * pair, 2 * pair + 1):
+                    cols = slice(half * 64, (half + 1) * 64)
+                    quantize("", grouped[:, t * HALF : (t + 1) * HALF], w1_mx[t][0][:, cols], w1_mx[t][1][:, cols])
 
-        a_grouped0 = group_plain("a_grouped0", a_raw[0], "scalar")
+        group_angles(0, "scalar")
+        group_angles(1, "scalar")
 
         h_banks = [psum.tile([P, S], F32, name="h_bank%d" % t, tag="bank%d" % t) for t in range(PACK)]
         h = [sb.tile([P, S], F32, name="h%d" % t) for t in range(PACK)]
@@ -120,15 +139,22 @@ def tile_picked_dime_silu_e_kernel(tc, xT, aT, w1, w3, w2, offs, pos1, pos2, out
             product(h_banks[t][:], w1_mx[t], slice(0, P), x_mx)
             nc.scalar.activation(out=h[t][:], in_=h_banks[t][:], func=SILU)
 
-        a_grouped1 = group_plain("a_grouped1", a_raw[1], "vector")
         a_mx = mx_tiles("a", S)
-        w3_grouped = sb.tile([P, PACK, P, PACK], BF16, name="w3_grouped", tag="w3_then_picked", align_bytes=64)
-        nc.scalar.copy(
-            out=w3_grouped[:].rearrange("p t m j -> p m j t"),
-            in_=w3_raw[:].rearrange("p j (m t) -> p m j t", t=PACK),
-        )
+        group_angles(2, "vector")
+        quantize("", a_grouped[0][:].rearrange("p q c -> p (q c)"), a_mx[0][:, 0:HALF], a_mx[1][:, 0:HALF])
+        group_angles(3, "scalar")
+        w3_grouped = []
+        for pair in range(2):
+            grouped = sb.tile(
+                [P, 2, P, PACK], BF16, name="w3_grouped%d" % pair, tag="after_w3_%d" % pair, align_bytes=64
+            )
+            nc.scalar.copy(
+                out=grouped[:].rearrange("p t m j -> p m j t"),
+                in_=w3_raw[:].rearrange("p j (m t) -> p m j t", t=PACK)[:, :, :, 2 * pair : 2 * pair + 2],
+            )
+            w3_grouped.append(grouped)
         w2_grouped = group_plain("w2_grouped", w2_raw, "scalar")
-        w3_mx = [mx_tiles("w3_%d" % t, P) for t in range(PACK)]
+        w3_mx = [mx_tiles("w3_%d" % pair, 2 * P) for pair in range(2)]
 
         picked = [sb.tile([P, 2 * V], F32, name="picked%d" % t) for t in range(PACK - 1)]
 
@@ -136,20 +162,22 @@ def tile_picked_dime_silu_e_kernel(tc, xT, aT, w1, w3, w2, offs, pos1, pos2, out
             nc.vector.tensor_copy(picked[t][:, 0:V], h[t][:].indirect(pos1_sb[:]))
             nc.vector.tensor_copy(picked[t][:, V : 2 * V], h[t][:].indirect(pos2_sb[:]))
 
+        def quantize_w3(pair):
+            quantize("", w3_grouped[pair][:].rearrange("p t m j -> p (t m j)"), w3_mx[pair][0][:], w3_mx[pair][1][:])
+
         fetch(0)
-        quantize("", a_grouped0[:], a_mx[0][:, 0:HALF], a_mx[1][:, 0:HALF])
-        quantize("", a_grouped1[:], a_mx[0][:, HALF:S], a_mx[1][:, HALF:S])
+        quantize("", a_grouped[1][:].rearrange("p q c -> p (q c)"), a_mx[0][:, HALF:S], a_mx[1][:, HALF:S])
         fetch(1)
         fetch(2)
-        for t in range(PACK):
-            quantize("", w3_grouped[:, t, :, :].rearrange("p m j -> p (m j)"), w3_mx[t][0][:], w3_mx[t][1][:])
-        picked.append(sb.tile([P, 2 * V], F32, name="picked3", tag="w3_then_picked", align_bytes=64))
+        quantize_w3(0)
+        picked.append(sb.tile([P, 2 * V], F32, name="picked3", tag="after_w3_0", align_bytes=64))
         fetch(3)
+        quantize_w3(1)
 
         f_banks = [psum.tile([P, S], F32, name="f_bank%d" % t, tag="bank%d" % (PACK + t)) for t in range(PACK)]
-        terms = sb.tile([P, PACK, 2 * V], F32, name="terms")
+        terms = sb.tile([P, PACK, 2 * V], F32, name="terms", tag="after_w3_1", align_bytes=64)
         for t in range(PACK):
-            product(f_banks[t][:], w3_mx[t], slice(0, P), a_mx)
+            product(f_banks[t][:], w3_mx[t // 2], slice((t % 2) * P, (t % 2 + 1) * P), a_mx)
             nc.vector.tensor_tensor(terms[:, t, :], picked[t][:], f_banks[t][:], MULT)
 
         w2_mx = mx_tiles("w2", N)

@@ -95,7 +95,7 @@ def tile_picked_dime_silu_e_kernel(tc, xT, aT, w1, w3, w2, offs, pos1, pos2, out
         a_rows = aT.rearrange("(p j) c -> p j c", j=PACK)
         a_raw = [sb.tile([P, PACK, P], F32, name="a_raw%d" % q) for q in range(4)]
         for q in range(4):
-            if q == 2:
+            if q == 3:
                 nc.sync.dma_start(pos1_sb[:], pos1)
                 nc.sync.dma_start(pos2_sb[:], pos2)
             nc.sync.dma_start(out=a_raw[q][:], in_=a_rows[:, :, q * P : (q + 1) * P])
@@ -117,11 +117,19 @@ def tile_picked_dime_silu_e_kernel(tc, xT, aT, w1, w3, w2, offs, pos1, pos2, out
         nc.scalar.activation(out=warm[:, 8:9], in_=warm[:, 0:1], func=SILU)
 
         x_grouped = sb.tile([P, S, PACK], BF16, name="x_grouped", align_bytes=64)
-        for j in range(PACK):
+        last = PACK - 1
+        for j in range(last):
             nc.vector.tensor_copy(x_grouped[:, :, j], x_planes[j][:].indirect(offs_sb[:]))
+        for half in range(2):
+            nc.vector.tensor_copy(
+                x_grouped[:, half * HALF : (half + 1) * HALF, last],
+                x_planes[last][:].indirect(offs_sb[:, half * 16 : (half + 1) * 16]),
+            )
         w1_grouped0 = group_dealt("w1_grouped0", w1_raw[0], "scalar")
         x_mx = mx_tiles("x", S)
-        quantize("", x_grouped[:].rearrange("p s j -> p (s j)"), x_mx[0][:], x_mx[1][:])
+        for half in range(2):
+            cols = slice(half * HALF, (half + 1) * HALF)
+            quantize("", x_grouped[:, cols, :].rearrange("p s j -> p (s j)"), x_mx[0][:, cols], x_mx[1][:, cols])
         w1_grouped1 = group_dealt("w1_grouped1", w1_raw[1], "vector")
         w1_mx = [mx_tiles("w1_%d" % t, P) for t in range(PACK)]
         for pair in range(2):
@@ -187,9 +195,9 @@ def tile_picked_dime_silu_e_kernel(tc, xT, aT, w1, w3, w2, offs, pos1, pos2, out
         z_grouped = [sb.tile([P, VH * PACK], BF16, name="z_grouped%d" % half, align_bytes=64) for half in range(2)]
         for half in range(2):
             nc.vector.tensor_tensor(
-                z_grouped[half][:].rearrange("p (c i t) -> p c t i", i=4, t=PACK),
-                terms[:, :, half * VH : (half + 1) * VH].rearrange("p t (c i) -> p c t i", i=4),
-                terms[:, :, V + half * VH : V + (half + 1) * VH].rearrange("p t (c i) -> p c t i", i=4),
+                z_grouped[half][:].rearrange("p (c i t) -> p c t i", i=2, t=PACK),
+                terms[:, :, half * VH : (half + 1) * VH].rearrange("p t (c i) -> p c t i", i=2),
+                terms[:, :, V + half * VH : V + (half + 1) * VH].rearrange("p t (c i) -> p c t i", i=2),
                 ADD,
             )
         out_rows = out.rearrange("(u p) v -> p u v", p=P)
@@ -201,4 +209,5 @@ def tile_picked_dime_silu_e_kernel(tc, xT, aT, w1, w3, w2, offs, pos1, pos2, out
                 product(o_bank[:, u, :], w2_mx, slice(u * P, (u + 1) * P), z_mx)
             result = sb.tile([P, N // P, VH], F32, name="result%d" % half)
             nc.scalar.activation(out=result[:], in_=o_bank[:], func=SILU)
-            nc.sync.dma_start(out=out_rows[:, :, half * VH : (half + 1) * VH], in_=result[:])
+            queue = nc.sync if half == 0 else nc.scalar
+            queue.dma_start(out=out_rows[:, :, half * VH : (half + 1) * VH], in_=result[:])

@@ -92,24 +92,23 @@ def tile_picked_dime_silu_e_kernel(tc, xT, aT, w1, w3, w2, offs, pos1, pos2, out
         for j in range(1, PACK):
             nc.sync.dma_start(out=x_planes[j][:], in_=x_rows[:, j, :])
         w1_raw = [load_half("w1", w1, half) for half in range(2)]
-        a_rows = aT.rearrange("(p j) c -> p j c", j=PACK)
-        a_raw = [sb.tile([P, PACK, P], F32, name="a_raw%d" % q) for q in range(4)]
+        w3_rows = w3.rearrange("(p j) c -> p j c", j=PACK)
+        w3_raw = [sb.tile([P, PACK, P], F32, name="w3_raw%d" % q) for q in range(4)]
         for q in range(4):
             if q == 3:
                 nc.sync.dma_start(pos1_sb[:], pos1)
                 nc.sync.dma_start(pos2_sb[:], pos2)
-            nc.sync.dma_start(out=a_raw[q][:], in_=a_rows[:, :, q * P : (q + 1) * P])
-        a_grouped = [sb.tile([P, 2, P * PACK], BF16, name="a_grouped%d" % d, align_bytes=64) for d in range(2)]
+            nc.sync.dma_start(out=w3_raw[q][:], in_=w3_rows[:, :, q * P : (q + 1) * P])
+        w3_grouped = [sb.tile([P, PACK, 64, PACK], BF16, name="w3_grouped%d" % half, align_bytes=64) for half in range(2)]
 
-        def group_angles(q, engine):
+        def group_w3(q, engine):
             copy_on(
                 engine,
-                a_grouped[q // 2][:, q % 2, :].rearrange("p (c i j) -> p c j i", i=4, j=PACK),
-                a_raw[q][:].rearrange("p j (c i) -> p c j i", i=4),
+                w3_grouped[q // 2][:, :, (q % 2) * 32 : (q % 2 + 1) * 32, :].rearrange("p t m j -> p m j t"),
+                w3_raw[q][:].rearrange("p j (m t) -> p m j t", t=PACK),
             )
 
-        w3_raw = sb.tile([P, PACK, H], F32, name="w3_raw")
-        nc.sync.dma_start(out=w3_raw[:], in_=w3.rearrange("(p j) c -> p j c", j=PACK))
+        a_raw = [load_half("a", aT, half) for half in range(2)]
         w2_raw = load_half("w2", w2, 0)
 
         warm = sb.tile([P, 16], F32, name="warm")
@@ -138,66 +137,88 @@ def tile_picked_dime_silu_e_kernel(tc, xT, aT, w1, w3, w2, offs, pos1, pos2, out
                     cols = slice(half * 64, (half + 1) * 64)
                     quantize("", grouped[:, t * HALF : (t + 1) * HALF], w1_mx[t][0][:, cols], w1_mx[t][1][:, cols])
 
-        group_angles(0, "scalar")
-        group_angles(1, "scalar")
+        group_w3(0, "scalar")
+        group_w3(1, "scalar")
 
         h_banks = [psum.tile([P, S], F32, name="h_bank%d" % t, tag="bank%d" % t) for t in range(PACK)]
         h = [sb.tile([P, S], F32, name="h%d" % t) for t in range(PACK)]
         for t in range(PACK):
             product(h_banks[t][:], w1_mx[t], slice(0, P), x_mx)
+        for t in range(PACK):
             nc.scalar.activation(out=h[t][:], in_=h_banks[t][:], func=SILU)
 
-        a_mx = mx_tiles("a", S)
-        group_angles(2, "vector")
-        quantize("", a_grouped[0][:].rearrange("p q c -> p (q c)"), a_mx[0][:, 0:HALF], a_mx[1][:, 0:HALF])
-        group_angles(3, "scalar")
-        w3_grouped = []
-        for pair in range(2):
-            grouped = sb.tile(
-                [P, 2, P, PACK], BF16, name="w3_grouped%d" % pair, tag="after_w3_%d" % pair, align_bytes=64
-            )
-            nc.scalar.copy(
-                out=grouped[:].rearrange("p t m j -> p m j t"),
-                in_=w3_raw[:].rearrange("p j (m t) -> p m j t", t=PACK)[:, :, :, 2 * pair : 2 * pair + 2],
-            )
-            w3_grouped.append(grouped)
-        w2_grouped = group_plain("w2_grouped", w2_raw, "scalar")
-        w3_mx = [mx_tiles("w3_%d" % pair, 2 * P) for pair in range(2)]
+        w3_mx = [mx_tiles("w3_%d" % t, P) for t in range(PACK)]
 
-        picked = [sb.tile([P, 2 * V], F32, name="picked%d" % t) for t in range(PACK - 1)]
+        def quantize_w3(half):
+            cols = slice(half * 64, (half + 1) * 64)
+            for t in range(PACK):
+                quantize(
+                    "",
+                    w3_grouped[half][:, t, :, :].rearrange("p m j -> p (m j)"),
+                    w3_mx[t][0][:, cols],
+                    w3_mx[t][1][:, cols],
+                )
 
-        def fetch(t):
-            nc.vector.tensor_copy(picked[t][:, 0:V], h[t][:].indirect(pos1_sb[:]))
-            nc.vector.tensor_copy(picked[t][:, V : 2 * V], h[t][:].indirect(pos2_sb[:]))
-
-        def quantize_w3(pair):
-            quantize("", w3_grouped[pair][:].rearrange("p t m j -> p (t m j)"), w3_mx[pair][0][:], w3_mx[pair][1][:])
-
-        fetch(0)
-        quantize("", a_grouped[1][:].rearrange("p q c -> p (q c)"), a_mx[0][:, HALF:S], a_mx[1][:, HALF:S])
-        fetch(1)
-        fetch(2)
         quantize_w3(0)
-        picked.append(sb.tile([P, 2 * V], F32, name="picked3", tag="after_w3_0", align_bytes=64))
-        fetch(3)
-        quantize_w3(1)
+        group_w3(2, "vector")
+        group_w3(3, "scalar")
+        shared0 = sb.tile([P, 3 * V], F32, name="shared0", align_bytes=64)
+        shared1 = sb.tile([P, 2 * PACK * V], F32, name="shared1", align_bytes=64)
+        a_grouped = [shared0[:, V : 3 * V].bitcast(BF16), shared1[:, V : 3 * V].bitcast(BF16)]
+        for d in range(2):
+            nc.scalar.copy(
+                out=a_grouped[d].rearrange("p (c i j) -> p c j i", i=4, j=PACK),
+                in_=a_raw[d][:].rearrange("p j (c i) -> p c j i", i=4),
+            )
+        w2_grouped = group_plain("w2_grouped", w2_raw, "scalar")
 
-        f_banks = [psum.tile([P, S], F32, name="f_bank%d" % t, tag="bank%d" % (PACK + t)) for t in range(PACK)]
-        terms = sb.tile([P, PACK, 2 * V], F32, name="terms", tag="after_w3_1", align_bytes=64)
-        for t in range(PACK):
-            product(f_banks[t][:], w3_mx[t // 2], slice((t % 2) * P, (t % 2 + 1) * P), a_mx)
-            nc.vector.tensor_tensor(terms[:, t, :], picked[t][:], f_banks[t][:], MULT)
+        picked00 = sb.tile([P, 2 * V], F32, name="picked00")
+        picked10 = sb.tile([P, 2 * V], F32, name="picked10", tag="picked1_0", align_bytes=64)
+        picked11 = sb.tile([P, 2 * V], F32, name="picked11")
+        picked = [[picked00[:], shared0[:, 0 : 2 * V]], [picked10[:], picked11[:]]]
 
-        w2_mx = mx_tiles("w2", N)
+        def fetch(t, d):
+            places = (pos1_sb, pos2_sb)[d]
+            nc.vector.tensor_copy(picked[d][t // 2][:, (t % 2) * V : (t % 2 + 1) * V], h[t][:].indirect(places[:]))
+
+        a_mx = [mx_tiles("a%d" % d, V) for d in range(2)]
+
+        def quantize_angles(d):
+            for half in range(2):
+                cols = slice(half * P, (half + 1) * P)
+                quantize("", a_grouped[d][:, half * S : (half + 1) * S], a_mx[d][0][:, cols], a_mx[d][1][:, cols])
+
+        for t in range(last):
+            fetch(t, 0)
+            fetch(t, 1)
+            if t == 1:
+                quantize_w3(1)
+        fetch(last, 1)
+        quantize_angles(0)
+        fetch(last, 0)
+        quantize_angles(1)
+
+        terms = shared1[:].rearrange("p (d t v) -> p d t v", d=2, t=PACK)
+        for d in range(2):
+            for pair in range(2):
+                f_bank = psum.tile([P, 2 * V], F32, name="f_bank%d_%d" % (d, pair), tag="bank%d" % (PACK + 2 * d + pair))
+                for i in range(2):
+                    product(f_bank[:, i * V : (i + 1) * V], w3_mx[2 * pair + i], slice(0, P), a_mx[d])
+                first = (2 * d + pair) * 2 * V
+                nc.vector.tensor_tensor(shared1[:, first : first + 2 * V], picked[d][pair], f_bank[:], MULT)
+
+        w2_codes = sb.tile([P, N], U32, name="w2_codes", tag="picked1_0", align_bytes=64)
+        w2_scales = sb.tile([P, N], U8, name="w2_scales", align_bytes=64)
+        w2_mx = (w2_codes, w2_scales)
         quantize("", w2_grouped[:], w2_mx[0][:], w2_mx[1][:])
 
         VH = V // 2
         z_grouped = [sb.tile([P, VH * PACK], BF16, name="z_grouped%d" % half, align_bytes=64) for half in range(2)]
         for half in range(2):
             nc.vector.tensor_tensor(
-                z_grouped[half][:].rearrange("p (c i t) -> p c t i", i=2, t=PACK),
-                terms[:, :, half * VH : (half + 1) * VH].rearrange("p t (c i) -> p c t i", i=2),
-                terms[:, :, V + half * VH : V + (half + 1) * VH].rearrange("p t (c i) -> p c t i", i=2),
+                z_grouped[half][:].rearrange("p (c i t) -> p c t i", i=4, t=PACK),
+                terms[:, 0, :, half * VH : (half + 1) * VH].rearrange("p t (c i) -> p c t i", i=4),
+                terms[:, 1, :, half * VH : (half + 1) * VH].rearrange("p t (c i) -> p c t i", i=4),
                 ADD,
             )
         out_rows = out.rearrange("(u p) v -> p u v", p=P)

@@ -3,7 +3,7 @@ from contextlib import ExitStack
 import concourse.mybir as mybir
 
 K, T, S, V, H, N = 512, 2048, 512, 256, 512, 256
-FLOPS = 2 * K * H * S + 2 * K * H * S + 2 * H * N * V
+FLOPS = 2 * K * H * S + 2 * K * H * 2 * V + 2 * H * N * V
 
 F32 = mybir.dt.float32
 BF16 = mybir.dt.bfloat16
@@ -17,7 +17,12 @@ ADD = mybir.AluOpType.add
 
 P = 128
 PACK = 4
-HALF = 256
+LAST = PACK - 1
+RUN = 4
+LIST_ROWS = 16
+PIECE = 256
+W3_PIECE = 128
+M_HALF = P // 2
 
 
 def tile_picked_dime_silu_e_kernel(tc, xT, aT, w1, w3, w2, offs, pos1, pos2, out):
@@ -28,117 +33,103 @@ def tile_picked_dime_silu_e_kernel(tc, xT, aT, w1, w3, w2, offs, pos1, pos2, out
         sb = ctx.enter_context(tc.tile_pool(name="sb", bufs=1))
         psum = ctx.enter_context(tc.psum_pool(name="psum", bufs=1))
 
-        def quantize(name, grouped, codes, scales):
-            nc.vector.quantize_mx(out=codes.bitcast(FP8X4), scales=scales, in_=grouped)
-
         def mx_tiles(name, width):
-            codes = sb.tile([P, width], U32, name=name + "_codes", align_bytes=64)
+            words = sb.tile([P, width], U32, name=name + "_words", align_bytes=64)
             scales = sb.tile([P, width], U8, name=name + "_scales", align_bytes=64)
-            return codes, scales
+            return words, scales
 
-        def product(acc, lhs, lhs_cols, rhs):
+        def quantize(grouped, operand, cols):
+            words, scales = operand
+            nc.vector.quantize_mx(out=words[:, cols].bitcast(FP8X4), scales=scales[:, cols], in_=grouped)
+
+        def product(acc, stationary, cols, moving):
             nc.tensor.matmul_mx(
                 out=acc,
-                lhsT=lhs[0][:, lhs_cols].bitcast(FP8X4),
-                lhsT_scale=lhs[1][:, lhs_cols],
-                rhs=rhs[0][:].bitcast(FP8X4),
-                rhs_scale=rhs[1][:],
+                lhsT=stationary[0][:, cols].bitcast(FP8X4),
+                lhsT_scale=stationary[1][:, cols],
+                rhs=moving[0][:].bitcast(FP8X4),
+                rhs_scale=moving[1][:],
                 start=True,
                 stop=True,
             )
 
-        def load_half(name, src, half):
-            raw = sb.tile([P, PACK, HALF], F32, name="%s_raw%d" % (name, half))
-            nc.sync.dma_start(
-                out=raw[:], in_=src.rearrange("(p j) c -> p j c", j=PACK)[:, :, half * HALF : (half + 1) * HALF]
-            )
+        def load_columns(name, matrix, piece, width):
+            raw = sb.tile([P, PACK, width], F32, name="%s_raw%d" % (name, piece))
+            rows = matrix.rearrange("(p j) c -> p j c", j=PACK)
+            nc.sync.dma_start(out=raw[:], in_=rows[:, :, piece * width : (piece + 1) * width])
             return raw
 
-        def copy_on(engine, dst, src):
-            if engine == "scalar":
-                nc.scalar.copy(out=dst, in_=src)
-            else:
-                nc.vector.tensor_copy(out=dst, in_=src)
-
-        def group_plain(name, raw, engine):
-            grouped = sb.tile([P, HALF * PACK], BF16, name=name, align_bytes=64)
-            copy_on(
-                engine,
-                grouped[:].rearrange("p (c i j) -> p c j i", i=4, j=PACK),
-                raw[:].rearrange("p j (c i) -> p c j i", i=4),
+        def group_plain(grouped, raw):
+            nc.scalar.copy(
+                out=grouped.rearrange("p (c i j) -> p c j i", i=RUN, j=PACK),
+                in_=raw[:].rearrange("p j (c i) -> p c j i", i=RUN),
             )
-            return grouped
 
-        def group_dealt(name, raw, engine):
-            grouped = sb.tile([P, HALF * PACK], BF16, name=name, align_bytes=64)
-            copy_on(
-                engine,
-                grouped[:].rearrange("p (t m j) -> p m j t", t=PACK, j=PACK),
-                raw[:].rearrange("p j (m t) -> p m j t", t=PACK),
-            )
-            return grouped
+        def group_dealt(copy, grouped, raw):
+            copy(out=grouped.rearrange("p t m j -> p m j t"), in_=raw[:].rearrange("p j (m t) -> p m j t", t=PACK))
 
-        def quantize_dealt(grouped, half, t, target):
-            cols = slice(t * P + half * 64, t * P + (half + 1) * 64)
-            quantize("", grouped[:, t * HALF : (t + 1) * HALF], target[0][:, cols], target[1][:, cols])
+        def quantize_dealt(grouped, operands, half, t):
+            cols = slice(half * M_HALF, (half + 1) * M_HALF)
+            quantize(grouped[:, t, :, :].rearrange("p m j -> p (m j)"), operands[t], cols)
 
-        x_rows = xT.rearrange("(p j) c -> p j c", j=PACK)
-        x_planes = [sb.tile([P, T], F32, name="x_plane%d" % j) for j in range(PACK)]
-        offs_sb = lists.tile([P, S // 16], U16, name="offs_sb")
-        pos1_sb = lists.tile([P, V // 16], U16, name="pos1_sb")
-        pos2_sb = lists.tile([P, V // 16], U16, name="pos2_sb")
-        nc.sync.dma_start(out=x_planes[0][:], in_=x_rows[:, 0, :])
+        xT_rows = xT.rearrange("(p j) c -> p j c", j=PACK)
+        x_rows = [sb.tile([P, T], F32, name="x_rows%d" % j) for j in range(PACK)]
+        offs_sb = lists.tile([P, S // LIST_ROWS], U16, name="offs_sb")
+        pos1_sb = lists.tile([P, V // LIST_ROWS], U16, name="pos1_sb")
+        pos2_sb = lists.tile([P, V // LIST_ROWS], U16, name="pos2_sb")
+        nc.sync.dma_start(out=x_rows[0][:], in_=xT_rows[:, 0, :])
         nc.sync.dma_start(offs_sb[:], offs)
         for j in range(1, PACK):
-            nc.sync.dma_start(out=x_planes[j][:], in_=x_rows[:, j, :])
-        w1_raw = [load_half("w1", w1, half) for half in range(2)]
-        w3_rows = w3.rearrange("(p j) c -> p j c", j=PACK)
-        w3_raw = [sb.tile([P, PACK, P], F32, name="w3_raw%d" % q) for q in range(4)]
-        for q in range(4):
-            if q == 3:
-                nc.sync.dma_start(pos1_sb[:], pos1)
-                nc.sync.dma_start(pos2_sb[:], pos2)
-            nc.sync.dma_start(out=w3_raw[q][:], in_=w3_rows[:, :, q * P : (q + 1) * P])
-        w3_grouped = [sb.tile([P, PACK, 64, PACK], BF16, name="w3_grouped%d" % half, align_bytes=64) for half in range(2)]
-
-        def group_w3(q, engine):
-            copy_on(
-                engine,
-                w3_grouped[q // 2][:, :, (q % 2) * 32 : (q % 2 + 1) * 32, :].rearrange("p t m j -> p m j t"),
-                w3_raw[q][:].rearrange("p j (m t) -> p m j t", t=PACK),
-            )
-
-        a_raw = [load_half("a", aT, half) for half in range(2)]
-        w2_raw = load_half("w2", w2, 0)
+            nc.sync.dma_start(out=x_rows[j][:], in_=xT_rows[:, j, :])
+        w1_raw = [load_columns("w1", w1, half, PIECE) for half in range(2)]
+        w3_raw = [load_columns("w3", w3, piece, W3_PIECE) for piece in range(3)]
+        nc.sync.dma_start(pos1_sb[:], pos1)
+        nc.sync.dma_start(pos2_sb[:], pos2)
+        w3_raw.append(load_columns("w3", w3, 3, W3_PIECE))
+        a_raw = [load_columns("a", aT, d, V) for d in range(2)]
+        w2_raw = load_columns("w2", w2, 0, N)
 
         warm = sb.tile([P, 16], F32, name="warm")
         nc.vector.memset(warm[:, 0:1], 0.0)
         nc.scalar.activation(out=warm[:, 8:9], in_=warm[:, 0:1], func=SILU)
 
         x_grouped = sb.tile([P, S, PACK], BF16, name="x_grouped", align_bytes=64)
-        last = PACK - 1
-        for j in range(last):
-            nc.vector.tensor_copy(x_grouped[:, :, j], x_planes[j][:].indirect(offs_sb[:]))
-        for half in range(2):
-            nc.vector.tensor_copy(
-                x_grouped[:, half * HALF : (half + 1) * HALF, last],
-                x_planes[last][:].indirect(offs_sb[:, half * 16 : (half + 1) * 16]),
-            )
-        w1_grouped0 = group_dealt("w1_grouped0", w1_raw[0], "scalar")
+        for j in range(LAST):
+            nc.vector.tensor_copy(x_grouped[:, :, j], x_rows[j][:].indirect(offs_sb[:]))
+        list_halves = [slice(half * S // 2, (half + 1) * S // 2) for half in range(2)]
+        for entries in list_halves:
+            offsets = offs_sb[:, entries.start // LIST_ROWS : entries.stop // LIST_ROWS]
+            nc.vector.tensor_copy(x_grouped[:, entries, LAST], x_rows[LAST][:].indirect(offsets))
+
+        w1_grouped = [
+            sb.tile([P, PACK, M_HALF, PACK], BF16, name="w1_grouped%d" % half, align_bytes=64) for half in range(2)
+        ]
+        group_dealt(nc.scalar.copy, w1_grouped[0][:], w1_raw[0])
         x_mx = mx_tiles("x", S)
-        for half in range(2):
-            cols = slice(half * HALF, (half + 1) * HALF)
-            quantize("", x_grouped[:, cols, :].rearrange("p s j -> p (s j)"), x_mx[0][:, cols], x_mx[1][:, cols])
-        w1_grouped1 = group_dealt("w1_grouped1", w1_raw[1], "vector")
+        for entries in list_halves:
+            quantize(x_grouped[:, entries, :].rearrange("p s j -> p (s j)"), x_mx, entries)
+        group_dealt(nc.vector.tensor_copy, w1_grouped[1][:], w1_raw[1])
         w1_mx = [mx_tiles("w1_%d" % t, P) for t in range(PACK)]
         for pair in range(2):
-            for half, grouped in enumerate((w1_grouped0, w1_grouped1)):
+            for half in range(2):
                 for t in (2 * pair, 2 * pair + 1):
-                    cols = slice(half * 64, (half + 1) * 64)
-                    quantize("", grouped[:, t * HALF : (t + 1) * HALF], w1_mx[t][0][:, cols], w1_mx[t][1][:, cols])
+                    quantize_dealt(w1_grouped[half], w1_mx, half, t)
 
-        group_w3(0, "scalar")
-        group_w3(1, "scalar")
+        w3_grouped = [
+            sb.tile([P, PACK, M_HALF, PACK], BF16, name="w3_grouped%d" % half, align_bytes=64) for half in range(2)
+        ]
+        w3_mx = [mx_tiles("w3_%d" % t, P) for t in range(PACK)]
+
+        def group_w3(copy, piece):
+            m_count = W3_PIECE // PACK
+            m_first = (piece % 2) * m_count
+            group_dealt(copy, w3_grouped[piece // 2][:, :, m_first : m_first + m_count, :], w3_raw[piece])
+
+        def quantize_w3(half):
+            for t in range(PACK):
+                quantize_dealt(w3_grouped[half], w3_mx, half, t)
+
+        group_w3(nc.scalar.copy, 0)
 
         h_banks = [psum.tile([P, S], F32, name="h_bank%d" % t, tag="bank%d" % t) for t in range(PACK)]
         h = [sb.tile([P, S], F32, name="h%d" % t) for t in range(PACK)]
@@ -147,88 +138,78 @@ def tile_picked_dime_silu_e_kernel(tc, xT, aT, w1, w3, w2, offs, pos1, pos2, out
         for t in range(PACK):
             nc.scalar.activation(out=h[t][:], in_=h_banks[t][:], func=SILU)
 
-        w3_mx = [mx_tiles("w3_%d" % t, P) for t in range(PACK)]
-
-        def quantize_w3(half):
-            cols = slice(half * 64, (half + 1) * 64)
-            for t in range(PACK):
-                quantize(
-                    "",
-                    w3_grouped[half][:, t, :, :].rearrange("p m j -> p (m j)"),
-                    w3_mx[t][0][:, cols],
-                    w3_mx[t][1][:, cols],
-                )
-
+        group_w3(nc.vector.tensor_copy, 1)
         quantize_w3(0)
-        group_w3(2, "vector")
-        group_w3(3, "scalar")
-        shared0 = sb.tile([P, 3 * V], F32, name="shared0", align_bytes=64)
-        shared1 = sb.tile([P, 2 * PACK * V], F32, name="shared1", align_bytes=64)
-        a_grouped = [shared0[:, V : 3 * V].bitcast(BF16), shared1[:, V : 3 * V].bitcast(BF16)]
+        group_w3(nc.vector.tensor_copy, 2)
+
+        picked_late = sb.tile([P, 3 * V], F32, name="picked_late", align_bytes=64)
+        terms = sb.tile([P, 2 * PACK * V], F32, name="terms", align_bytes=64)
+        a_grouped = [picked_late[:, V : 3 * V].bitcast(BF16), terms[:, V : 3 * V].bitcast(BF16)]
         for d in range(2):
-            nc.scalar.copy(
-                out=a_grouped[d].rearrange("p (c i j) -> p c j i", i=4, j=PACK),
-                in_=a_raw[d][:].rearrange("p j (c i) -> p c j i", i=4),
-            )
-        w2_grouped = group_plain("w2_grouped", w2_raw, "scalar")
+            group_plain(a_grouped[d], a_raw[d])
+        w2_grouped = sb.tile([P, N * PACK], BF16, name="w2_grouped", align_bytes=64)
+        group_plain(w2_grouped[:], w2_raw)
 
         picked00 = sb.tile([P, 2 * V], F32, name="picked00")
-        picked10 = sb.tile([P, 2 * V], F32, name="picked10", tag="picked1_0", align_bytes=64)
+        picked10 = sb.tile([P, 2 * V], F32, name="picked10", tag="picked10_then_w2", align_bytes=64)
         picked11 = sb.tile([P, 2 * V], F32, name="picked11")
-        picked = [[picked00[:], shared0[:, 0 : 2 * V]], [picked10[:], picked11[:]]]
+        picked = [[picked00[:], picked_late[:, 0 : 2 * V]], [picked10[:], picked11[:]]]
+        places = [pos1_sb, pos2_sb]
 
         def fetch(t, d):
-            places = (pos1_sb, pos2_sb)[d]
-            nc.vector.tensor_copy(picked[d][t // 2][:, (t % 2) * V : (t % 2 + 1) * V], h[t][:].indirect(places[:]))
+            nc.vector.tensor_copy(picked[d][t // 2][:, (t % 2) * V : (t % 2 + 1) * V], h[t][:].indirect(places[d][:]))
 
         a_mx = [mx_tiles("a%d" % d, V) for d in range(2)]
 
         def quantize_angles(d):
-            for half in range(2):
-                cols = slice(half * P, (half + 1) * P)
-                quantize("", a_grouped[d][:, half * S : (half + 1) * S], a_mx[d][0][:, cols], a_mx[d][1][:, cols])
+            for cols in (slice(0, V // 2), slice(V // 2, V)):
+                quantize(a_grouped[d][:, cols.start * PACK : cols.stop * PACK], a_mx[d], cols)
 
-        for t in range(last):
-            fetch(t, 0)
-            fetch(t, 1)
-            if t == 1:
-                quantize_w3(1)
-        fetch(last, 1)
+        for d in range(2):
+            fetch(0, d)
+        group_w3(nc.vector.tensor_copy, 3)
+        for d in range(2):
+            fetch(1, d)
+        quantize_w3(1)
+        for d in range(2):
+            fetch(2, d)
+        fetch(LAST, 1)
         quantize_angles(0)
-        fetch(last, 0)
+        fetch(LAST, 0)
         quantize_angles(1)
 
-        terms = shared1[:].rearrange("p (d t v) -> p d t v", d=2, t=PACK)
         for d in range(2):
             for pair in range(2):
-                f_bank = psum.tile([P, 2 * V], F32, name="f_bank%d_%d" % (d, pair), tag="bank%d" % (PACK + 2 * d + pair))
-                for i in range(2):
-                    product(f_bank[:, i * V : (i + 1) * V], w3_mx[2 * pair + i], slice(0, P), a_mx[d])
-                first = (2 * d + pair) * 2 * V
-                nc.vector.tensor_tensor(shared1[:, first : first + 2 * V], picked[d][pair], f_bank[:], MULT)
+                step = 2 * d + pair
+                f_bank = psum.tile([P, 2 * V], F32, name="f_bank%d" % step, tag="bank%d" % (PACK + step))
+                for side in range(2):
+                    product(f_bank[:, side * V : (side + 1) * V], w3_mx[2 * pair + side], slice(0, P), a_mx[d])
+                nc.vector.tensor_tensor(terms[:, step * 2 * V : (step + 1) * 2 * V], picked[d][pair], f_bank[:], MULT)
 
-        w2_codes = sb.tile([P, N], U32, name="w2_codes", tag="picked1_0", align_bytes=64)
+        w2_words = sb.tile([P, N], U32, name="w2_words", tag="picked10_then_w2", align_bytes=64)
         w2_scales = sb.tile([P, N], U8, name="w2_scales", align_bytes=64)
-        w2_mx = (w2_codes, w2_scales)
-        quantize("", w2_grouped[:], w2_mx[0][:], w2_mx[1][:])
+        w2_mx = (w2_words, w2_scales)
+        quantize(w2_grouped[:], w2_mx, slice(0, N))
 
-        VH = V // 2
-        z_grouped = [sb.tile([P, VH * PACK], BF16, name="z_grouped%d" % half, align_bytes=64) for half in range(2)]
-        for half in range(2):
+        terms_dtv = terms[:].rearrange("p (d t v) -> p d t v", d=2, t=PACK)
+        target_halves = [slice(half * V // 2, (half + 1) * V // 2) for half in range(2)]
+        z_grouped = [sb.tile([P, V // 2 * PACK], BF16, name="z_grouped%d" % half, align_bytes=64) for half in range(2)]
+        for half, targets in enumerate(target_halves):
             nc.vector.tensor_tensor(
-                z_grouped[half][:].rearrange("p (c i t) -> p c t i", i=4, t=PACK),
-                terms[:, 0, :, half * VH : (half + 1) * VH].rearrange("p t (c i) -> p c t i", i=4),
-                terms[:, 1, :, half * VH : (half + 1) * VH].rearrange("p t (c i) -> p c t i", i=4),
+                z_grouped[half][:].rearrange("p (c i t) -> p c t i", i=RUN, t=PACK),
+                terms_dtv[:, 0, :, targets].rearrange("p t (c i) -> p c t i", i=RUN),
+                terms_dtv[:, 1, :, targets].rearrange("p t (c i) -> p c t i", i=RUN),
                 ADD,
             )
+
         out_rows = out.rearrange("(u p) v -> p u v", p=P)
-        for half in range(2):
-            z_mx = mx_tiles("z%d" % half, VH)
-            quantize("", z_grouped[half][:], z_mx[0][:], z_mx[1][:])
-            o_bank = psum.tile([P, N // P, VH], F32, name="o_bank%d" % half, tag="bank%d" % half)
+        for half, targets in enumerate(target_halves):
+            z_mx = mx_tiles("z%d" % half, V // 2)
+            quantize(z_grouped[half][:], z_mx, slice(0, V // 2))
+            out_bank = psum.tile([P, N // P, V // 2], F32, name="out_bank%d" % half, tag="bank%d" % half)
             for u in range(N // P):
-                product(o_bank[:, u, :], w2_mx, slice(u * P, (u + 1) * P), z_mx)
-            result = sb.tile([P, N // P, VH], F32, name="result%d" % half)
-            nc.scalar.activation(out=result[:], in_=o_bank[:], func=SILU)
-            queue = nc.sync if half == 0 else nc.scalar
-            queue.dma_start(out=out_rows[:, :, half * VH : (half + 1) * VH], in_=result[:])
+                product(out_bank[:, u, :], w2_mx, slice(u * P, (u + 1) * P), z_mx)
+            result = sb.tile([P, N // P, V // 2], F32, name="result%d" % half)
+            nc.scalar.activation(out=result[:], in_=out_bank[:], func=SILU)
+            queue = (nc.sync, nc.scalar)[half]
+            queue.dma_start(out=out_rows[:, :, targets], in_=result[:])

from contextlib import ExitStack

import concourse.mybir as mybir

K, T, S, V, H, N = 512, 2048, 512, 256, 512, 256
FLOPS = 2 * K * H * S + 2 * K * H * 2 * V + 2 * H * N * V

F32 = mybir.dt.float32
BF16 = mybir.dt.bfloat16
U32 = mybir.dt.uint32
U16 = mybir.dt.uint16
U8 = mybir.dt.uint8
FP8X4 = mybir.dt.float8_e4m3fn_x4
SILU = mybir.ActivationFunctionType.Silu
MULT = mybir.AluOpType.mult
ADD = mybir.AluOpType.add

P = 128
PACK = 4
LAST = PACK - 1
RUN = 4
LIST_ROWS = 16
PIECE = 256
W3_PIECE = 128
M_HALF = P // 2


def tile_picked_dime_silu_e_kernel(tc, xT, aT, w1, w3, w2, offs, pos1, pos2, out):
    nc = tc.nc

    with ExitStack() as ctx:
        lists = ctx.enter_context(tc.tile_pool(name="lists", bufs=1))
        sb = ctx.enter_context(tc.tile_pool(name="sb", bufs=1))
        psum = ctx.enter_context(tc.psum_pool(name="psum", bufs=1))

        def mx_tiles(name, width):
            words = sb.tile([P, width], U32, name=name + "_words", align_bytes=64)
            scales = sb.tile([P, width], U8, name=name + "_scales", align_bytes=64)
            return words, scales

        def quantize(grouped, operand, cols):
            words, scales = operand
            nc.vector.quantize_mx(out=words[:, cols].bitcast(FP8X4), scales=scales[:, cols], in_=grouped)

        def product(acc, stationary, cols, moving):
            nc.tensor.matmul_mx(
                out=acc,
                lhsT=stationary[0][:, cols].bitcast(FP8X4),
                lhsT_scale=stationary[1][:, cols],
                rhs=moving[0][:].bitcast(FP8X4),
                rhs_scale=moving[1][:],
                start=True,
                stop=True,
            )

        def load_columns(name, matrix, piece, width):
            raw = sb.tile([P, PACK, width], F32, name="%s_raw%d" % (name, piece))
            rows = matrix.rearrange("(p j) c -> p j c", j=PACK)
            nc.sync.dma_start(out=raw[:], in_=rows[:, :, piece * width : (piece + 1) * width])
            return raw

        def group_plain(grouped, raw):
            nc.scalar.copy(
                out=grouped.rearrange("p (c i j) -> p c j i", i=RUN, j=PACK),
                in_=raw[:].rearrange("p j (c i) -> p c j i", i=RUN),
            )

        def group_dealt(copy, grouped, raw):
            copy(out=grouped.rearrange("p t m j -> p m j t"), in_=raw[:].rearrange("p j (m t) -> p m j t", t=PACK))

        def quantize_dealt(grouped, operands, half, t):
            cols = slice(half * M_HALF, (half + 1) * M_HALF)
            quantize(grouped[:, t, :, :].rearrange("p m j -> p (m j)"), operands[t], cols)

        xT_rows = xT.rearrange("(p j) c -> p j c", j=PACK)
        x_rows = [sb.tile([P, T], F32, name="x_rows%d" % j) for j in range(PACK)]
        offs_sb = lists.tile([P, S // LIST_ROWS], U16, name="offs_sb")
        pos1_sb = lists.tile([P, V // LIST_ROWS], U16, name="pos1_sb")
        pos2_sb = lists.tile([P, V // LIST_ROWS], U16, name="pos2_sb")
        nc.sync.dma_start(out=x_rows[0][:], in_=xT_rows[:, 0, :])
        nc.sync.dma_start(offs_sb[:], offs)
        for j in range(1, PACK):
            nc.sync.dma_start(out=x_rows[j][:], in_=xT_rows[:, j, :])
        w1_raw = [load_columns("w1", w1, half, PIECE) for half in range(2)]
        w3_raw = [load_columns("w3", w3, piece, W3_PIECE) for piece in range(3)]
        nc.sync.dma_start(pos1_sb[:], pos1)
        nc.sync.dma_start(pos2_sb[:], pos2)
        w3_raw.append(load_columns("w3", w3, 3, W3_PIECE))
        a_raw = [load_columns("a", aT, d, V) for d in range(2)]
        w2_raw = load_columns("w2", w2, 0, N)

        warm = sb.tile([P, 16], F32, name="warm")
        nc.vector.memset(warm[:, 0:1], 0.0)
        nc.scalar.activation(out=warm[:, 8:9], in_=warm[:, 0:1], func=SILU)

        x_grouped = sb.tile([P, S, PACK], BF16, name="x_grouped", align_bytes=64)
        for j in range(LAST):
            nc.vector.tensor_copy(x_grouped[:, :, j], x_rows[j][:].indirect(offs_sb[:]))
        list_halves = [slice(half * S // 2, (half + 1) * S // 2) for half in range(2)]
        for entries in list_halves:
            offsets = offs_sb[:, entries.start // LIST_ROWS : entries.stop // LIST_ROWS]
            nc.vector.tensor_copy(x_grouped[:, entries, LAST], x_rows[LAST][:].indirect(offsets))

        w1_grouped = [
            sb.tile([P, PACK, M_HALF, PACK], BF16, name="w1_grouped%d" % half, align_bytes=64) for half in range(2)
        ]
        group_dealt(nc.scalar.copy, w1_grouped[0][:], w1_raw[0])
        x_mx = mx_tiles("x", S)
        for entries in list_halves:
            quantize(x_grouped[:, entries, :].rearrange("p s j -> p (s j)"), x_mx, entries)
        group_dealt(nc.vector.tensor_copy, w1_grouped[1][:], w1_raw[1])
        w1_mx = [mx_tiles("w1_%d" % t, P) for t in range(PACK)]
        for pair in range(2):
            for half in range(2):
                for t in (2 * pair, 2 * pair + 1):
                    quantize_dealt(w1_grouped[half], w1_mx, half, t)

        w3_grouped = [
            sb.tile([P, PACK, M_HALF, PACK], BF16, name="w3_grouped%d" % half, align_bytes=64) for half in range(2)
        ]
        w3_mx = [mx_tiles("w3_%d" % t, P) for t in range(PACK)]

        def group_w3(copy, piece):
            m_count = W3_PIECE // PACK
            m_first = (piece % 2) * m_count
            group_dealt(copy, w3_grouped[piece // 2][:, :, m_first : m_first + m_count, :], w3_raw[piece])

        def quantize_w3(half):
            for t in range(PACK):
                quantize_dealt(w3_grouped[half], w3_mx, half, t)

        group_w3(nc.scalar.copy, 0)

        h_banks = [psum.tile([P, S], F32, name="h_bank%d" % t, tag="bank%d" % t) for t in range(PACK)]
        h = [sb.tile([P, S], F32, name="h%d" % t) for t in range(PACK)]
        for t in range(PACK):
            product(h_banks[t][:], w1_mx[t], slice(0, P), x_mx)
        for t in range(PACK):
            nc.scalar.activation(out=h[t][:], in_=h_banks[t][:], func=SILU)

        group_w3(nc.vector.tensor_copy, 1)
        quantize_w3(0)
        group_w3(nc.vector.tensor_copy, 2)

        picked_late = sb.tile([P, 3 * V], F32, name="picked_late", align_bytes=64)
        terms = sb.tile([P, 2 * PACK * V], F32, name="terms", align_bytes=64)
        a_grouped = [picked_late[:, V : 3 * V].bitcast(BF16), terms[:, V : 3 * V].bitcast(BF16)]
        for d in range(2):
            group_plain(a_grouped[d], a_raw[d])
        w2_grouped = sb.tile([P, N * PACK], BF16, name="w2_grouped", align_bytes=64)
        group_plain(w2_grouped[:], w2_raw)

        picked00 = sb.tile([P, 2 * V], F32, name="picked00")
        picked10 = sb.tile([P, 2 * V], F32, name="picked10", tag="picked10_then_w2", align_bytes=64)
        picked11 = sb.tile([P, 2 * V], F32, name="picked11")
        picked = [[picked00[:], picked_late[:, 0 : 2 * V]], [picked10[:], picked11[:]]]
        places = [pos1_sb, pos2_sb]

        def fetch(t, d):
            nc.vector.tensor_copy(picked[d][t // 2][:, (t % 2) * V : (t % 2 + 1) * V], h[t][:].indirect(places[d][:]))

        a_mx = [mx_tiles("a%d" % d, V) for d in range(2)]

        def quantize_angles(d):
            for cols in (slice(0, V // 2), slice(V // 2, V)):
                quantize(a_grouped[d][:, cols.start * PACK : cols.stop * PACK], a_mx[d], cols)

        for d in range(2):
            fetch(0, d)
        group_w3(nc.vector.tensor_copy, 3)
        for d in range(2):
            fetch(1, d)
        quantize_w3(1)
        for d in range(2):
            fetch(2, d)
        fetch(LAST, 1)
        quantize_angles(0)
        fetch(LAST, 0)
        quantize_angles(1)

        for d in range(2):
            for pair in range(2):
                step = 2 * d + pair
                f_bank = psum.tile([P, 2 * V], F32, name="f_bank%d" % step, tag="bank%d" % (PACK + step))
                for side in range(2):
                    product(f_bank[:, side * V : (side + 1) * V], w3_mx[2 * pair + side], slice(0, P), a_mx[d])
                nc.vector.tensor_tensor(terms[:, step * 2 * V : (step + 1) * 2 * V], picked[d][pair], f_bank[:], MULT)

        w2_words = sb.tile([P, N], U32, name="w2_words", tag="picked10_then_w2", align_bytes=64)
        w2_scales = sb.tile([P, N], U8, name="w2_scales", align_bytes=64)
        w2_mx = (w2_words, w2_scales)
        quantize(w2_grouped[:], w2_mx, slice(0, N))

        terms_dtv = terms[:].rearrange("p (d t v) -> p d t v", d=2, t=PACK)
        target_halves = [slice(half * V // 2, (half + 1) * V // 2) for half in range(2)]
        z_grouped = [sb.tile([P, V // 2 * PACK], BF16, name="z_grouped%d" % half, align_bytes=64) for half in range(2)]
        for half, targets in enumerate(target_halves):
            nc.vector.tensor_tensor(
                z_grouped[half][:].rearrange("p (c i t) -> p c t i", i=RUN, t=PACK),
                terms_dtv[:, 0, :, targets].rearrange("p t (c i) -> p c t i", i=RUN),
                terms_dtv[:, 1, :, targets].rearrange("p t (c i) -> p c t i", i=RUN),
                ADD,
            )

        out_rows = out.rearrange("(u p) v -> p u v", p=P)
        for half, targets in enumerate(target_halves):
            z_mx = mx_tiles("z%d" % half, V // 2)
            quantize(z_grouped[half][:], z_mx, slice(0, V // 2))
            out_bank = psum.tile([P, N // P, V // 2], F32, name="out_bank%d" % half, tag="bank%d" % half)
            for u in range(N // P):
                product(out_bank[:, u, :], w2_mx, slice(u * P, (u + 1) * P), z_mx)
            result = sb.tile([P, N // P, V // 2], F32, name="result%d" % half)
            nc.scalar.activation(out=result[:], in_=out_bank[:], func=SILU)
            queue = (nc.sync, nc.scalar)[half]
            queue.dma_start(out=out_rows[:, :, targets], in_=result[:])
